import numpy as np
import ml_dtypes


def mxq(x, axis, fmt="e4m3"):
    dtype, down = {"e4m3": (ml_dtypes.float8_e4m3fn, 7), "e5m2": (ml_dtypes.float8_e5m2, 14)}[fmt]
    v = np.moveaxis(np.asarray(x, np.float32).astype(ml_dtypes.bfloat16).astype(np.float64), axis, -1)
    blocks = v.reshape(v.shape[:-1] + (-1, 32))
    amax = np.abs(blocks).max(-1, keepdims=True)
    byte = np.maximum(np.where(amax > 0, np.frexp(amax)[1] - 1 + 127, 0) - down, 1)
    scale = np.exp2(byte - 127.0)
    codes = (blocks / scale).astype(np.float32).astype(dtype).astype(np.float64)
    return np.moveaxis((codes * scale).reshape(v.shape), -1, axis)


WIDE = False


def mx_kscale(k):
    if not WIDE:
        return np.ones(k)
    levels = np.array([10, -10, 5, -5, 0])
    if k % 512:
        return np.exp2(np.random.permutation(np.resize(levels, k // 32))).repeat(32)
    a = np.empty((k // 512, 16))
    for p in range(k // 512):
        a[p, :8] = np.random.permutation(np.resize(levels, 8))
        for g in range(8):
            far = levels[np.abs(levels - a[p, g]) >= 10]
            a[p, g + 8] = far[np.random.randint(len(far))]
    return np.exp2(a.ravel()).repeat(32)


def f64(x):
    return np.asarray(x).astype(np.float64)


def striped(idx):
    return np.tile(idx.reshape(-1, 16).T, (8, 1)).astype(np.uint16)


def unstriped(offs):
    return offs[:16].T.reshape(-1).astype(np.int64)


E2M1 = np.array([0.0, 0.5, 1.0, 1.5, 2.0, 3.0, 4.0, 6.0, -0.0, -0.5, -1.0, -1.5, -2.0, -3.0, -4.0, -6.0])


def pack_weight(w, fmt):
    k, n = w.shape
    w = f64(np.asarray(w, np.float32).astype(ml_dtypes.bfloat16)).reshape(k // 32, 32, n)
    amax = np.abs(w).max(1)
    if fmt == "e4m3":
        byte = np.frexp(amax)[1] - 1 + 127 - 7
    else:
        mant, ex = np.frexp(amax / 6.0)
        byte = np.where(mant > 0.5, ex, ex - 1) + 127
    byte = np.clip(np.where(amax > 0, byte, 1), 1, 254)
    scaled = (w * np.exp2(127.0 - byte)[:, None, :]).reshape(k, n).astype(np.float32)
    by_word = np.ascontiguousarray(scaled.reshape(k // 512, 128, 4, n).transpose(0, 1, 3, 2))
    if fmt == "e4m3":
        words = by_word.astype(ml_dtypes.float8_e4m3fn).view(np.uint8)
    else:
        c = by_word.astype(ml_dtypes.float4_e2m1fn).view(np.uint8) & 0xF
        words = (c[..., 0::2] | (c[..., 1::2] << 4)).reshape(k // 512, 128, 2 * n)
    return np.ascontiguousarray(words), np.ascontiguousarray(byte.astype(np.uint8).reshape(k // 512, 16, n))


def unpack_weight(words, scales, fmt):
    g, _, n = scales.shape
    words = np.ascontiguousarray(words).reshape(g, 128, n, -1)
    if fmt == "e4m3":
        vals = words.view(ml_dtypes.float8_e4m3fn).astype(np.float64)
    else:
        nib = np.empty((g, 128, n, 4), np.uint8)
        nib[..., 0::2] = words & 0xF
        nib[..., 1::2] = words >> 4
        vals = E2M1[nib]
    vals = vals * np.repeat(np.exp2(scales.astype(np.float64) - 127.0), 8, axis=1)[..., None]
    return vals.transpose(0, 1, 3, 2).reshape(g * 512, n)


def relu(v):
    return np.maximum(v, 0.0)


def sigmoid(v):
    return 1.0 / (1.0 + np.exp(-np.maximum(v, -700.0)))


K, T, E, C, H, N = 512, 640, 10, 128, 512, 512


def by_expert(wq, xq):
    return np.concatenate([wq[e].T @ xq[:, e * C:(e + 1) * C] for e in range(E)], axis=1)


def setup_inputs():
    n = np.random.standard_normal
    s = mx_kscale(K)
    u = mx_kscale(H)
    first = np.random.permutation(np.repeat(np.arange(E), T // E))
    second = (first + 1 + np.random.permutation(np.repeat(np.arange(E - 1), -(-T // (E - 1)))[:T])) % E
    while np.bincount(second, minlength=E).max() != T // E:
        load = np.bincount(second, minlength=E); hi, lo = int(load.argmax()), int(load.argmin())
        t = np.flatnonzero((second == hi) & (first != lo))[0]; second[t] = lo
    slot_token = np.empty(E * C, np.int64); pos = np.empty((2, T), np.int64); fill = np.zeros(E, np.int64)
    place = np.stack([np.random.permutation(C) for _ in range(E)])
    for r, deal in enumerate((first, second)):
        for t in np.random.permutation(T):
            e = deal[t]; j = e * C + place[e, fill[e]]; fill[e] += 1; slot_token[j] = t; pos[r, t] = j
    g = np.random.uniform(0.2, 0.8, T)
    x = pack_weight(n((K, T)) * s[:, None], "e4m3")
    return {
        "x_words": x[0],
        "x_scales": x[1],
        "wg": (n((K, N)) / np.sqrt(K) / s[:, None]).astype(np.float32),
        "w1": (n((E, K, H)) / np.sqrt(K) / s[None, :, None] * u).astype(np.float32),
        "w2": (n((E, H, N)) / np.sqrt(H) / u[None, :, None]).astype(np.float32),
        "gate": np.stack([np.tile(g, (128, 1)), np.tile(1.0 - g, (128, 1))]).astype(np.float32),
        "offs": striped(slot_token),
        "pos1": striped(pos[0]),
        "pos2": striped(pos[1]),
    }


def reference(x_words, x_scales, wg, w1, w2, gate, offs, pos1, pos2):
    wgq = mxq(f64(wg), 0, "e4m3")
    w1q = mxq(f64(w1), 1, "e4m3")
    w2q = mxq(f64(w2), 1, "e4m3")
    idx = unstriped(offs)
    x = unpack_weight(x_words, x_scales, "e4m3")
    o = sigmoid(wgq.T @ x)
    h = relu(by_expert(w1q, x[:, idx]))
    y = by_expert(w2q, mxq(h, 0, "e4m3"))
    c = sum(f64(gate[r, :1]) * y[:, unstriped(p)] for r, p in enumerate((pos1, pos2)))
    return o * c

@@ -1,0 +1,211 @@
+from contextlib import ExitStack
+
+import concourse.mybir as mybir
+
+K, T, E, C, H, N = 512, 640, 10, 128, 512, 512
+S = E * C
+FLOPS = 2 * K * N * T + 2 * K * H * S + 2 * H * N * S
+
+F32 = mybir.dt.float32
+BF16 = mybir.dt.bfloat16
+I32 = mybir.dt.int32
+U32 = mybir.dt.uint32
+U16 = mybir.dt.uint16
+U8 = mybir.dt.uint8
+FP8X4 = mybir.dt.float8_e4m3fn_x4
+ACT = mybir.ActivationFunctionType
+MULT = mybir.AluOpType.mult
+ADD = mybir.AluOpType.add
+
+P = 128
+NT = N // P
+GATHER = 256
+W1_SCALAR_M = 96
+
+
+def tile_moe_ogt_relu_sigmoid_kernel(
+    tc, x_words, x_scales, wg, w1, w2, gate, offs, pos1, pos2, out
+):
+    nc = tc.nc
+    with ExitStack() as ctx:
+        keep = ctx.enter_context(tc.tile_pool(name="keep", bufs=1))
+        ring = ctx.enter_context(tc.tile_pool(name="ring", bufs=2))
+        psum = ctx.enter_context(tc.psum_pool(name="psum", bufs=2))
+
+        offs_t = keep.tile([P, S // 16], U16, name="offs_t")
+        pos_t = [keep.tile([P, T // 16], U16, name=f"pos_t{r}") for r in range(2)]
+        xw = keep.tile([P, T], I32, name="xw", align_bytes=64)
+        xs = keep.tile([P, T], U8, name="xs", align_bytes=64)
+        xgw = keep.tile([P, S], U32, name="xgw", align_bytes=64)
+        xgs = keep.tile([P, S], U8, name="xgs", align_bytes=64)
+        hw = keep.tile([P, S], U32, name="hw", align_bytes=64)
+        hs = keep.tile([P, S], U8, name="hs", align_bytes=64)
+        g = keep.tile([P, 2, T], F32, name="g")
+        o = keep.tile([P, NT, T], F32, name="o")
+        og = keep.tile([P, NT, 2, T], F32, name="og")
+        warm = keep.tile([P, 8], F32, name="warm")
+        warm2 = keep.tile([P, 8], F32, name="warm2")
+
+        nc.vector.memset(xs[:].bitcast(I32), 0)
+        nc.vector.memset(warm[:], 0.0)
+        nc.scalar.activation(warm2[:], warm[:], ACT.Sigmoid)
+
+        def load_full(w):
+            raw = ring.tile([P, 4, 512], F32, name="raw1", tag="raw1", bufs=6)
+            nc.sync.dma_start(raw[:], w.rearrange("(p j) n -> p j n", j=4))
+            return raw
+
+        def new_raw2():
+            return ring.tile([P, 4, 2 * P], F32, name="raw2", tag="raw2", bufs=12)
+
+        def load_w2(raw, i, e, j):
+            nc.sync.dma_start(
+                raw[:, :, i * P : (i + 1) * P],
+                w2[e].rearrange("(p j) n -> p j n", j=4)[:, :, j * P : (j + 1) * P],
+            )
+
+        nc.sync.dma_start(xw[:], x_words[0].rearrange("p t d -> p (t d)").bitcast(I32))
+        nc.sync.dma_start(offs_t[:], offs)
+        scale_rows = x_scales[0].bitcast(I32).rearrange("(q r) n -> r q n", r=4)
+        for r in range(4):
+            nc.scalar.dma_start(xs[r:P:32, :].bitcast(I32), scale_rows[r])
+        raw_g = load_full(wg)
+        raw1 = {}
+        raw2 = {}
+        for e in range(E):
+            raw1[e] = load_full(w1[e])
+            if e == 0:
+                nc.sync.dma_start(g[:], gate.rearrange("r p t -> p r t"))
+            if e == 2:
+                nc.sync.dma_start(pos_t[0][:], pos1)
+                nc.sync.dma_start(pos_t[1][:], pos2)
+            if e % 2 == 1:
+                raw2[0, e // 2] = new_raw2()
+                for i in range(2):
+                    load_w2(raw2[0, e // 2], i, e - 1 + i, 0)
+        for j in range(1, NT):
+            for q in range(E // 2):
+                raw2[j, q] = new_raw2()
+                for i in range(2):
+                    load_w2(raw2[j, q], i, 2 * q + i, j)
+
+        def copy_on(engine, dst, src):
+            if engine == "vector":
+                nc.vector.tensor_copy(dst, src)
+            else:
+                nc.scalar.copy(dst, src)
+
+        def quantize(words, scales, src):
+            nc.vector.quantize_mx(out=words.bitcast(FP8X4), scales=scales, in_=src)
+
+        def matmul(dst, lw, ls, rw, rs):
+            nc.tensor.matmul_mx(
+                out=dst, lhsT=lw.bitcast(FP8X4), lhsT_scale=ls, rhs=rw.bitcast(FP8X4), rhs_scale=rs,
+                start=True, stop=True,
+            )
+
+        def gather_tokens(q):
+            cols = slice(q * GATHER, (q + 1) * GATHER)
+            lst = offs_t[:, q * GATHER // 16 : (q + 1) * GATHER // 16]
+            nc.vector.tensor_copy(xgw[:, cols], xw[:].bitcast(U32).indirect(lst))
+            nc.vector.tensor_copy(xgs[:, cols], xs[:].indirect(lst))
+
+        def output_gate():
+            b = ring.tile([P, 2048], BF16, name="b1", tag="b1", bufs=3, align_bytes=64)
+            nc.scalar.copy(
+                b[:].rearrange("p (c i j) -> p c j i", i=4, j=4),
+                raw_g[:].rearrange("p j (c i) -> p c j i", i=4),
+            )
+            words = ring.tile([P, 512], U32, name="c1", tag="c1", bufs=2, align_bytes=64)
+            scales = ring.tile([P, 512], U8, name="s1", tag="s1", bufs=2, align_bytes=64)
+            quantize(words[:], scales[:], b[:])
+            tail = psum.tile([P, NT, P], F32, name="zt", tag="zt", bufs=1)
+            for j in range(NT):
+                cols = slice(j * P, (j + 1) * P)
+                matmul(tail[:, j, :], words[:, cols], scales[:, cols], xw[:, 512:T], xs[:, 512:T])
+            nc.scalar.activation(o[:, :, 512:T], tail[:], ACT.Sigmoid)
+            for j in range(NT):
+                cols = slice(j * P, (j + 1) * P)
+                z = psum.tile([P, 512], F32, name="z", tag="z", bufs=2)
+                matmul(z[:], words[:, cols], scales[:, cols], xw[:, 0:512], xs[:, 0:512])
+                nc.scalar.activation(o[:, j, 0:512], z[:], ACT.Sigmoid)
+
+        def fold_gate(j, r):
+            nc.vector.tensor_tensor(og[:, j, r, :], o[:, j, :], g[:, r, :], MULT)
+
+        def first_layer(e):
+            b = ring.tile([P, 2048], BF16, name="b1", tag="b1", bufs=3, align_bytes=64)
+            dst = b[:].rearrange("p (t m j) -> p m j t", t=4, j=4)
+            src = raw1[e][:].rearrange("p j (m t) -> p m j t", t=4)
+            nc.scalar.copy(dst[:, 0:W1_SCALAR_M], src[:, 0:W1_SCALAR_M])
+            nc.vector.tensor_copy(dst[:, W1_SCALAR_M:P], src[:, W1_SCALAR_M:P])
+            words = ring.tile([P, 512], U32, name="c1", tag="c1", bufs=2, align_bytes=64)
+            scales = ring.tile([P, 512], U8, name="s1", tag="s1", bufs=2, align_bytes=64)
+            quantize(words[:], scales[:], b[:])
+            slots = slice(e * C, (e + 1) * C)
+            hp = psum.tile([P, 4, C], F32, name="hp", tag="hp", bufs=2)
+            for t in range(4):
+                cols = slice(t * P, (t + 1) * P)
+                matmul(hp[:, t, :], words[:, cols], scales[:, cols], xgw[:, slots], xgs[:, slots])
+            hb = ring.tile([P, C, 4], BF16, name="hb", tag="hb", bufs=3, align_bytes=64)
+            nc.scalar.activation(hb[:], hp[:].rearrange("p t n -> p n t"), ACT.Relu)
+            quantize(hw[:, slots], hs[:, slots], hb[:].rearrange("p n t -> p (n t)"))
+
+        def second_layer(y, j, q, i0, i1, engine):
+            width = (i1 - i0) * P
+            b = ring.tile([P, 4 * width], BF16, name="b2", tag="b2", bufs=4, align_bytes=64)
+            copy_on(
+                engine,
+                b[:].rearrange("p (c i j) -> p c j i", i=4, j=4),
+                raw2[j, q][:, :, i0 * P : i1 * P].rearrange("p j (c i) -> p c j i", i=4),
+            )
+            words = ring.tile([P, width], U32, name="c2", tag="c2", bufs=3, align_bytes=64)
+            scales = ring.tile([P, width], U8, name="s2", tag="s2", bufs=3, align_bytes=64)
+            quantize(words[:], scales[:], b[:])
+            yp = psum.tile([P, width], F32, name="yp", tag="yp", bufs=3)
+            for i in range(i1 - i0):
+                cols = slice(i * P, (i + 1) * P)
+                e = 2 * q + i0 + i
+                slots = slice(e * C, (e + 1) * C)
+                matmul(yp[:, cols], words[:, cols], scales[:, cols], hw[:, slots], hs[:, slots])
+            nc.scalar.copy(y[:, (2 * q + i0) * C : (2 * q + i1) * C], yp[:])
+
+        def combine(y, j, t0, t1):
+            parts = []
+            for r in range(2):
+                part = ring.tile([P, t1 - t0], F32, name=f"part{r}", tag=f"part{r}", bufs=2)
+                lst = pos_t[r][:, t0 // 16 : t1 // 16]
+                nc.vector.tensor_tensor(part[:], y[:].indirect(lst), og[:, j, r, t0:t1], MULT)
+                parts.append(part)
+            res = ring.tile([P, t1 - t0], F32, name="res", tag="res", bufs=3)
+            nc.vector.tensor_tensor(res[:], parts[0][:], parts[1][:], ADD)
+            nc.sync.dma_start(out[j * P : (j + 1) * P, t0:t1], res[:])
+
+        def new_y():
+            return ring.tile([P, S], F32, name="y", tag="y", bufs=3)
+
+        gather_tokens(0)
+        output_gate()
+        y = new_y()
+        folds = [(j, r) for j in range(NT) for r in range(2)]
+        for q in range(E // 2):
+            first_layer(2 * q)
+            if q + 1 < E // 2:
+                gather_tokens(q + 1)
+            first_layer(2 * q + 1)
+            second_layer(y, 0, q, 0, 2, "vector")
+            for j, r in folds[2 * q : 2 * q + 2]:
+                fold_gate(j, r)
+
+        for j in range(1, NT):
+            done = y
+            y = new_y()
+            for q in range(E // 2):
+                if j == NT - 1 and q == E // 2 - 1:
+                    second_layer(y, j, q, 0, 1, "scalar")
+                    second_layer(y, j, q, 1, 2, "vector")
+                else:
+                    second_layer(y, j, q, 0, 2, "vector" if q == 2 else "scalar")
+            combine(done, j - 1, 0, T)
+        combine(y, NT - 1, 0, T // 2)
+        combine(y, NT - 1, T // 2, T)

@@ -20,7 +20,7 @@ ADD = mybir.AluOpType.add
 P = 128
 NT = N // P
 GATHER = 256
-W1_SCALAR_M = 96
+PRM = {"order": ["x", "offs", "g", "wg", ["a", 0], ["a", 1], ["a", 4], ["a", 2], ["a", 3], ["a", 5], ["a", 6], ["a", 8], ["a", 7], ["a", 9], ["b", 6], ["b", 2], ["b", 0], ["b", 1], ["b", 3], ["b", 4], ["b", 5], "p1", "p2", ["b", 8], ["b", 7], ["b", 9], ["b", 10], ["b", 11], ["b", 12], ["b", 13], ["b", 14], ["b", 15], ["b", 16], ["b", 17], ["b", 18], ["b", 19], ["b", 20], ["b", 21], ["b", 22], ["b", 23], ["b", 24], ["b", 25], ["b", 26], ["b", 27], ["b", 28], ["b", 29], ["b", 30], ["b", 31], ["b", 32], ["b", 33], ["b", 34], ["b", 35], ["b", 36], ["b", 37], ["b", 38], ["b", 39]], "mg": 128, "m": [96, 64, 80, 128, 80, 64, 64, 64, 64, 80], "relu": ["scalar", "scalar", "scalar", "scalar", "vector", "scalar", "scalar", "scalar", "scalar", "scalar"], "sizes": [4, 4, 4, 4, 4, 4, 4, 4, 4, 2, 1, 1], "f": [4, 4, 4, 0, 7, 8, 4, 7, 8, 0, 4, 8], "evac": ["scalar", "scalar", "scalar", "scalar", "scalar", "scalar", "scalar", "scalar", "scalar", "scalar", "scalar", "scalar"], "unit": [3, 4, 10, 6, 11, 11, 11, 11], "gated": [1, 1, 0, 1, 2, 2, 0, 0], "foldat": [1, 8, 1, 1, 1, 2, 10, 12], "oat": 0, "b1": 4, "c1": 4, "raw": 12, "text": [["x", 0], ["o"], ["a", 0], ["x", 1], ["a", 1], ["f", 0], ["f", 2], ["f", 3], ["f", 4], ["a", 2], ["x", 2], ["f", 5], ["a", 3], ["a", 4], ["x", 3], ["a", 5], ["a", 6], ["x", 4], ["a", 7], ["a", 8], ["f", 1], ["a", 9], ["b", 0], ["f", 6], ["b", 1], ["b", 2], ["f", 7], ["b", 3], ["c", 0, 1], ["b", 4], ["c", 1, 1], ["b", 5], ["b", 6], ["c", 3, 1], ["b", 7], ["b", 8], ["b", 9], ["b", 10], ["c", 2, 0], ["b", 11], ["c", 4, 2], ["c", 5, 0], ["c", 6, 0], ["c", 7, 0]]}
 
 
 def tile_moe_ogt_relu_sigmoid_kernel(
@@ -47,16 +47,14 @@ def tile_moe_ogt_relu_sigmoid_kernel(
         warm2 = keep.tile([P, 8], F32, name="warm2")
 
         nc.vector.memset(xs[:].bitcast(I32), 0)
-        nc.vector.memset(warm[:], 0.0)
-        nc.scalar.activation(warm2[:], warm[:], ACT.Sigmoid)
 
         def load_full(w):
-            raw = ring.tile([P, 4, 512], F32, name="raw1", tag="raw1", bufs=6)
+            raw = ring.tile([P, 4, 512], F32, name="raw1", tag="raw", bufs=PRM["raw"])
             nc.sync.dma_start(raw[:], w.rearrange("(p j) n -> p j n", j=4))
             return raw
 
         def new_raw2():
-            return ring.tile([P, 4, 2 * P], F32, name="raw2", tag="raw2", bufs=12)
+            return ring.tile([P, 4, 4 * P], F32, name="raw2", tag="raw", bufs=PRM["raw"])
 
         def load_w2(raw, i, e, j):
             nc.sync.dma_start(
@@ -64,30 +62,41 @@ def tile_moe_ogt_relu_sigmoid_kernel(
                 w2[e].rearrange("(p j) n -> p j n", j=4)[:, :, j * P : (j + 1) * P],
             )
 
-        nc.sync.dma_start(xw[:], x_words[0].rearrange("p t d -> p (t d)").bitcast(I32))
-        nc.sync.dma_start(offs_t[:], offs)
-        scale_rows = x_scales[0].bitcast(I32).rearrange("(q r) n -> r q n", r=4)
-        for r in range(4):
-            nc.scalar.dma_start(xs[r:P:32, :].bitcast(I32), scale_rows[r])
-        raw_g = load_full(wg)
+        scale_rows = x_scales[0].bitcast(I32)
+        for quad in range(4):
+            nc.scalar.dma_start(xs[32 * quad : 32 * quad + 4, :].bitcast(I32), scale_rows[4 * quad : 4 * quad + 4, :])
+        nc.vector.memset(warm[:], 0.0)
+        nc.scalar.activation(warm2[:], warm[:], ACT.Sigmoid)
+        groups = []
+        group_of = {}
+        for size in PRM["sizes"]:
+            first = sum(len(gr) for gr in groups)
+            groups.append(list(range(first, first + size)))
+            for i in range(size):
+                group_of[first + i] = (len(groups) - 1, i)
         raw1 = {}
         raw2 = {}
-        for e in range(E):
-            raw1[e] = load_full(w1[e])
-            if e == 0:
+        for item in PRM["order"]:
+            if item == "x":
+                nc.sync.dma_start(xw[:], x_words[0].rearrange("p t d -> p (t d)").bitcast(I32))
+            elif item == "offs":
+                nc.sync.dma_start(offs_t[:], offs)
+            elif item == "wg":
+                raw_g = load_full(wg)
+            elif item == "g":
                 nc.sync.dma_start(g[:], gate.rearrange("r p t -> p r t"))
-            if e == 2:
+            elif item == "p1":
                 nc.sync.dma_start(pos_t[0][:], pos1)
+            elif item == "p2":
                 nc.sync.dma_start(pos_t[1][:], pos2)
-            if e % 2 == 1:
-                raw2[0, e // 2] = new_raw2()
-                for i in range(2):
-                    load_w2(raw2[0, e // 2], i, e - 1 + i, 0)
-        for j in range(1, NT):
-            for q in range(E // 2):
-                raw2[j, q] = new_raw2()
-                for i in range(2):
-                    load_w2(raw2[j, q], i, 2 * q + i, j)
+            elif item[0] == "a":
+                raw1[item[1]] = load_full(w1[item[1]])
+            else:
+                piece = item[1]
+                k, i = group_of[piece]
+                if k not in raw2:
+                    raw2[k] = new_raw2()
+                load_w2(raw2[k], i, piece % E, piece // E)
 
         def copy_on(engine, dst, src):
             if engine == "vector":
@@ -111,14 +120,18 @@ def tile_moe_ogt_relu_sigmoid_kernel(
             nc.vector.tensor_copy(xgs[:, cols], xs[:].indirect(lst))
 
         def output_gate():
-            b = ring.tile([P, 2048], BF16, name="b1", tag="b1", bufs=3, align_bytes=64)
-            nc.scalar.copy(
-                b[:].rearrange("p (c i j) -> p c j i", i=4, j=4),
-                raw_g[:].rearrange("p j (c i) -> p c j i", i=4),
-            )
-            words = ring.tile([P, 512], U32, name="c1", tag="c1", bufs=2, align_bytes=64)
-            scales = ring.tile([P, 512], U8, name="s1", tag="s1", bufs=2, align_bytes=64)
-            quantize(words[:], scales[:], b[:])
+            stage = ring.tile([P, 1024], F32, name="b1", tag="b1", bufs=PRM["b1"], align_bytes=64)
+            b = stage[:].bitcast(BF16)
+            dst = b.rearrange("p (c i j) -> p c j i", i=4, j=4)
+            src = raw_g[:].rearrange("p j (c i) -> p c j i", i=4)
+            split = PRM["mg"]
+            if split > 0:
+                nc.scalar.copy(dst[:, 0:split], src[:, 0:split])
+            if split < P:
+                nc.vector.tensor_copy(dst[:, split:P], src[:, split:P])
+            words = ring.tile([P, 512], U32, name="c1", tag="c1", bufs=PRM["c1"], align_bytes=64)
+            scales = ring.tile([P, 512], U8, name="s1", tag="s1", bufs=PRM["c1"], align_bytes=64)
+            quantize(words[:], scales[:], b)
             tail = psum.tile([P, NT, P], F32, name="zt", tag="zt", bufs=1)
             for j in range(NT):
                 cols = slice(j * P, (j + 1) * P)
@@ -134,78 +147,94 @@ def tile_moe_ogt_relu_sigmoid_kernel(
             nc.vector.tensor_tensor(og[:, j, r, :], o[:, j, :], g[:, r, :], MULT)
 
         def first_layer(e):
-            b = ring.tile([P, 2048], BF16, name="b1", tag="b1", bufs=3, align_bytes=64)
-            dst = b[:].rearrange("p (t m j) -> p m j t", t=4, j=4)
+            stage = ring.tile([P, 1024], F32, name="b1", tag="b1", bufs=PRM["b1"], align_bytes=64)
+            b = stage[:].bitcast(BF16)
+            dst = b.rearrange("p (t m j) -> p m j t", t=4, j=4)
             src = raw1[e][:].rearrange("p j (m t) -> p m j t", t=4)
-            nc.scalar.copy(dst[:, 0:W1_SCALAR_M], src[:, 0:W1_SCALAR_M])
-            nc.vector.tensor_copy(dst[:, W1_SCALAR_M:P], src[:, W1_SCALAR_M:P])
-            words = ring.tile([P, 512], U32, name="c1", tag="c1", bufs=2, align_bytes=64)
-            scales = ring.tile([P, 512], U8, name="s1", tag="s1", bufs=2, align_bytes=64)
-            quantize(words[:], scales[:], b[:])
+            split = PRM["m"][e]
+            if split > 0:
+                nc.scalar.copy(dst[:, 0:split], src[:, 0:split])
+            if split < P:
+                nc.vector.tensor_copy(dst[:, split:P], src[:, split:P])
+            words = ring.tile([P, 512], U32, name="c1", tag="c1", bufs=PRM["c1"], align_bytes=64)
+            scales = ring.tile([P, 512], U8, name="s1", tag="s1", bufs=PRM["c1"], align_bytes=64)
+            quantize(words[:], scales[:], b)
             slots = slice(e * C, (e + 1) * C)
             hp = psum.tile([P, 4, C], F32, name="hp", tag="hp", bufs=2)
             for t in range(4):
                 cols = slice(t * P, (t + 1) * P)
                 matmul(hp[:, t, :], words[:, cols], scales[:, cols], xgw[:, slots], xgs[:, slots])
             hb = ring.tile([P, C, 4], BF16, name="hb", tag="hb", bufs=3, align_bytes=64)
-            nc.scalar.activation(hb[:], hp[:].rearrange("p t n -> p n t"), ACT.Relu)
+            if PRM["relu"][e] == "scalar":
+                nc.scalar.activation(hb[:], hp[:].rearrange("p t n -> p n t"), ACT.Relu)
+            else:
+                nc.vector.tensor_scalar_max(hb[:], hp[:].rearrange("p t n -> p n t"), 0.0)
             quantize(hw[:, slots], hs[:, slots], hb[:].rearrange("p n t -> p (n t)"))
+            return stage
 
-        def second_layer(y, j, q, i0, i1, engine):
-            width = (i1 - i0) * P
-            b = ring.tile([P, 4 * width], BF16, name="b2", tag="b2", bufs=4, align_bytes=64)
-            copy_on(
-                engine,
-                b[:].rearrange("p (c i j) -> p c j i", i=4, j=4),
-                raw2[j, q][:, :, i0 * P : i1 * P].rearrange("p j (c i) -> p c j i", i=4),
-            )
-            words = ring.tile([P, width], U32, name="c2", tag="c2", bufs=3, align_bytes=64)
-            scales = ring.tile([P, width], U8, name="s2", tag="s2", bufs=3, align_bytes=64)
-            quantize(words[:], scales[:], b[:])
+        def second_layer(k):
+            pieces = groups[k]
+            width = len(pieces) * P
+            stage = ring.tile([P, 1024], F32, name="b1", tag="b1", bufs=PRM["b1"], align_bytes=64)
+            b = stage[:, 0 : 2 * width].bitcast(BF16)
+            dst = b.rearrange("p (c i j) -> p c j i", i=4, j=4)
+            src = raw2[k][:, :, 0:width].rearrange("p j (c i) -> p c j i", i=4)
+            split = PRM["f"][k] * width // (4 * 8)
+            if split > 0:
+                nc.scalar.copy(dst[:, 0:split], src[:, 0:split])
+            if split < width // 4:
+                nc.vector.tensor_copy(dst[:, split : width // 4], src[:, split : width // 4])
+            words = ring.tile([P, width], U32, name="c1", tag="c1", bufs=PRM["c1"], align_bytes=64)
+            scales = ring.tile([P, width], U8, name="s1", tag="s1", bufs=PRM["c1"], align_bytes=64)
+            quantize(words[:], scales[:], b)
             yp = psum.tile([P, width], F32, name="yp", tag="yp", bufs=3)
-            for i in range(i1 - i0):
+            for i, piece in enumerate(pieces):
                 cols = slice(i * P, (i + 1) * P)
-                e = 2 * q + i0 + i
-                slots = slice(e * C, (e + 1) * C)
+                slots = slice(piece % E * C, (piece % E + 1) * C)
                 matmul(yp[:, cols], words[:, cols], scales[:, cols], hw[:, slots], hs[:, slots])
-            nc.scalar.copy(y[:, (2 * q + i0) * C : (2 * q + i1) * C], yp[:])
+            for j in sorted({piece // E for piece in pieces}):
+                mine = [i for i, piece in enumerate(pieces) if piece // E == j]
+                e0 = pieces[mine[0]] % E
+                if j not in ys:
+                    ys[j] = new_y()
+                copy_on(
+                    PRM["evac"][k],
+                    ys[j][:, e0 * C : (e0 + len(mine)) * C],
+                    yp[:, mine[0] * P : (mine[-1] + 1) * P],
+                )
+            return stage
 
-        def combine(y, j, t0, t1):
-            parts = []
+        half = T // 2
+
+        def combine(j, h, spent):
+            tokens = slice(h * half, (h + 1) * half)
+            if spent is None:
+                spent = ring.tile([P, T], F32, name="parts", tag="parts", bufs=2)
             for r in range(2):
-                part = ring.tile([P, t1 - t0], F32, name=f"part{r}", tag=f"part{r}", bufs=2)
-                lst = pos_t[r][:, t0 // 16 : t1 // 16]
-                nc.vector.tensor_tensor(part[:], y[:].indirect(lst), og[:, j, r, t0:t1], MULT)
-                parts.append(part)
-            res = ring.tile([P, t1 - t0], F32, name="res", tag="res", bufs=3)
-            nc.vector.tensor_tensor(res[:], parts[0][:], parts[1][:], ADD)
-            nc.sync.dma_start(out[j * P : (j + 1) * P, t0:t1], res[:])
+                lst = pos_t[r][:, h * half // 16 : (h + 1) * half // 16]
+                nc.vector.tensor_tensor(
+                    spent[:, r * half : (r + 1) * half], ys[j][:].indirect(lst), og[:, j, r, tokens], MULT
+                )
+            res = ring.tile([P, half], F32, name="res", tag="res", bufs=4)
+            nc.vector.tensor_tensor(res[:], spent[:, 0:half], spent[:, half:T], ADD)
+            nc.sync.dma_start(out[j * P : (j + 1) * P, tokens], res[:])
 
         def new_y():
             return ring.tile([P, S], F32, name="y", tag="y", bufs=3)
 
-        gather_tokens(0)
-        output_gate()
-        y = new_y()
+        ys = {}
+        spent = []
         folds = [(j, r) for j in range(NT) for r in range(2)]
-        for q in range(E // 2):
-            first_layer(2 * q)
-            if q + 1 < E // 2:
-                gather_tokens(q + 1)
-            first_layer(2 * q + 1)
-            second_layer(y, 0, q, 0, 2, "vector")
-            for j, r in folds[2 * q : 2 * q + 2]:
-                fold_gate(j, r)
-
-        for j in range(1, NT):
-            done = y
-            y = new_y()
-            for q in range(E // 2):
-                if j == NT - 1 and q == E // 2 - 1:
-                    second_layer(y, j, q, 0, 1, "scalar")
-                    second_layer(y, j, q, 1, 2, "vector")
-                else:
-                    second_layer(y, j, q, 0, 2, "vector" if q == 2 else "scalar")
-            combine(done, j - 1, 0, T)
-        combine(y, NT - 1, 0, T // 2)
-        combine(y, NT - 1, T // 2, T)
+        for step in PRM["text"]:
+            if step[0] == "x":
+                gather_tokens(step[1])
+            elif step[0] == "o":
+                output_gate()
+            elif step[0] == "a":
+                spent.append(first_layer(step[1]))
+            elif step[0] == "f":
+                fold_gate(folds[step[1]][0], folds[step[1]][1])
+            elif step[0] == "b":
+                spent.append(second_layer(step[1]))
+            elif step[0] == "c":
+                combine(step[1] // 2, step[1] % 2, spent[-step[2]] if step[2] else None)

from contextlib import ExitStack

import concourse.mybir as mybir

K, T, E, C, H, N = 512, 640, 10, 128, 512, 512
S = E * C
FLOPS = 2 * K * N * T + 2 * K * H * S + 2 * H * N * S

F32 = mybir.dt.float32
BF16 = mybir.dt.bfloat16
I32 = mybir.dt.int32
U32 = mybir.dt.uint32
U16 = mybir.dt.uint16
U8 = mybir.dt.uint8
FP8X4 = mybir.dt.float8_e4m3fn_x4
ACT = mybir.ActivationFunctionType
MULT = mybir.AluOpType.mult
ADD = mybir.AluOpType.add

P = 128
NT = N // P
GATHER = 256
PRM = {"order": ["x", "offs", "g", "wg", ["a", 0], ["a", 1], ["a", 4], ["a", 2], ["a", 3], ["a", 5], ["a", 6], ["a", 8], ["a", 7], ["a", 9], ["b", 6], ["b", 2], ["b", 0], ["b", 1], ["b", 3], ["b", 4], ["b", 5], "p1", "p2", ["b", 8], ["b", 7], ["b", 9], ["b", 10], ["b", 11], ["b", 12], ["b", 13], ["b", 14], ["b", 15], ["b", 16], ["b", 17], ["b", 18], ["b", 19], ["b", 20], ["b", 21], ["b", 22], ["b", 23], ["b", 24], ["b", 25], ["b", 26], ["b", 27], ["b", 28], ["b", 29], ["b", 30], ["b", 31], ["b", 32], ["b", 33], ["b", 34], ["b", 35], ["b", 36], ["b", 37], ["b", 38], ["b", 39]], "mg": 128, "m": [96, 64, 80, 128, 80, 64, 64, 64, 64, 80], "relu": ["scalar", "scalar", "scalar", "scalar", "vector", "scalar", "scalar", "scalar", "scalar", "scalar"], "sizes": [4, 4, 4, 4, 4, 4, 4, 4, 4, 2, 1, 1], "f": [4, 4, 4, 0, 7, 8, 4, 7, 8, 0, 4, 8], "evac": ["scalar", "scalar", "scalar", "scalar", "scalar", "scalar", "scalar", "scalar", "scalar", "scalar", "scalar", "scalar"], "unit": [3, 4, 10, 6, 11, 11, 11, 11], "gated": [1, 1, 0, 1, 2, 2, 0, 0], "foldat": [1, 8, 1, 1, 1, 2, 10, 12], "oat": 0, "b1": 4, "c1": 4, "raw": 12, "text": [["x", 0], ["o"], ["a", 0], ["x", 1], ["a", 1], ["f", 0], ["f", 2], ["f", 3], ["f", 4], ["a", 2], ["x", 2], ["f", 5], ["a", 3], ["a", 4], ["x", 3], ["a", 5], ["a", 6], ["x", 4], ["a", 7], ["a", 8], ["f", 1], ["a", 9], ["b", 0], ["f", 6], ["b", 1], ["b", 2], ["f", 7], ["b", 3], ["c", 0, 1], ["b", 4], ["c", 1, 1], ["b", 5], ["b", 6], ["c", 3, 1], ["b", 7], ["b", 8], ["b", 9], ["b", 10], ["c", 2, 0], ["b", 11], ["c", 4, 2], ["c", 5, 0], ["c", 6, 0], ["c", 7, 0]]}


def tile_moe_ogt_relu_sigmoid_kernel(
    tc, x_words, x_scales, wg, w1, w2, gate, offs, pos1, pos2, out
):
    nc = tc.nc
    with ExitStack() as ctx:
        keep = ctx.enter_context(tc.tile_pool(name="keep", bufs=1))
        ring = ctx.enter_context(tc.tile_pool(name="ring", bufs=2))
        psum = ctx.enter_context(tc.psum_pool(name="psum", bufs=2))

        offs_t = keep.tile([P, S // 16], U16, name="offs_t")
        pos_t = [keep.tile([P, T // 16], U16, name=f"pos_t{r}") for r in range(2)]
        xw = keep.tile([P, T], I32, name="xw", align_bytes=64)
        xs = keep.tile([P, T], U8, name="xs", align_bytes=64)
        xgw = keep.tile([P, S], U32, name="xgw", align_bytes=64)
        xgs = keep.tile([P, S], U8, name="xgs", align_bytes=64)
        hw = keep.tile([P, S], U32, name="hw", align_bytes=64)
        hs = keep.tile([P, S], U8, name="hs", align_bytes=64)
        g = keep.tile([P, 2, T], F32, name="g")
        o = keep.tile([P, NT, T], F32, name="o")
        og = keep.tile([P, NT, 2, T], F32, name="og")
        warm = keep.tile([P, 8], F32, name="warm")
        warm2 = keep.tile([P, 8], F32, name="warm2")

        nc.vector.memset(xs[:].bitcast(I32), 0)

        def load_full(w):
            raw = ring.tile([P, 4, 512], F32, name="raw1", tag="raw", bufs=PRM["raw"])
            nc.sync.dma_start(raw[:], w.rearrange("(p j) n -> p j n", j=4))
            return raw

        def new_raw2():
            return ring.tile([P, 4, 4 * P], F32, name="raw2", tag="raw", bufs=PRM["raw"])

        def load_w2(raw, i, e, j):
            nc.sync.dma_start(
                raw[:, :, i * P : (i + 1) * P],
                w2[e].rearrange("(p j) n -> p j n", j=4)[:, :, j * P : (j + 1) * P],
            )

        scale_rows = x_scales[0].bitcast(I32)
        for quad in range(4):
            nc.scalar.dma_start(xs[32 * quad : 32 * quad + 4, :].bitcast(I32), scale_rows[4 * quad : 4 * quad + 4, :])
        nc.vector.memset(warm[:], 0.0)
        nc.scalar.activation(warm2[:], warm[:], ACT.Sigmoid)
        groups = []
        group_of = {}
        for size in PRM["sizes"]:
            first = sum(len(gr) for gr in groups)
            groups.append(list(range(first, first + size)))
            for i in range(size):
                group_of[first + i] = (len(groups) - 1, i)
        raw1 = {}
        raw2 = {}
        for item in PRM["order"]:
            if item == "x":
                nc.sync.dma_start(xw[:], x_words[0].rearrange("p t d -> p (t d)").bitcast(I32))
            elif item == "offs":
                nc.sync.dma_start(offs_t[:], offs)
            elif item == "wg":
                raw_g = load_full(wg)
            elif item == "g":
                nc.sync.dma_start(g[:], gate.rearrange("r p t -> p r t"))
            elif item == "p1":
                nc.sync.dma_start(pos_t[0][:], pos1)
            elif item == "p2":
                nc.sync.dma_start(pos_t[1][:], pos2)
            elif item[0] == "a":
                raw1[item[1]] = load_full(w1[item[1]])
            else:
                piece = item[1]
                k, i = group_of[piece]
                if k not in raw2:
                    raw2[k] = new_raw2()
                load_w2(raw2[k], i, piece % E, piece // E)

        def copy_on(engine, dst, src):
            if engine == "vector":
                nc.vector.tensor_copy(dst, src)
            else:
                nc.scalar.copy(dst, src)

        def quantize(words, scales, src):
            nc.vector.quantize_mx(out=words.bitcast(FP8X4), scales=scales, in_=src)

        def matmul(dst, lw, ls, rw, rs):
            nc.tensor.matmul_mx(
                out=dst, lhsT=lw.bitcast(FP8X4), lhsT_scale=ls, rhs=rw.bitcast(FP8X4), rhs_scale=rs,
                start=True, stop=True,
            )

        def gather_tokens(q):
            cols = slice(q * GATHER, (q + 1) * GATHER)
            lst = offs_t[:, q * GATHER // 16 : (q + 1) * GATHER // 16]
            nc.vector.tensor_copy(xgw[:, cols], xw[:].bitcast(U32).indirect(lst))
            nc.vector.tensor_copy(xgs[:, cols], xs[:].indirect(lst))

        def output_gate():
            stage = ring.tile([P, 1024], F32, name="b1", tag="b1", bufs=PRM["b1"], align_bytes=64)
            b = stage[:].bitcast(BF16)
            dst = b.rearrange("p (c i j) -> p c j i", i=4, j=4)
            src = raw_g[:].rearrange("p j (c i) -> p c j i", i=4)
            split = PRM["mg"]
            if split > 0:
                nc.scalar.copy(dst[:, 0:split], src[:, 0:split])
            if split < P:
                nc.vector.tensor_copy(dst[:, split:P], src[:, split:P])
            words = ring.tile([P, 512], U32, name="c1", tag="c1", bufs=PRM["c1"], align_bytes=64)
            scales = ring.tile([P, 512], U8, name="s1", tag="s1", bufs=PRM["c1"], align_bytes=64)
            quantize(words[:], scales[:], b)
            tail = psum.tile([P, NT, P], F32, name="zt", tag="zt", bufs=1)
            for j in range(NT):
                cols = slice(j * P, (j + 1) * P)
                matmul(tail[:, j, :], words[:, cols], scales[:, cols], xw[:, 512:T], xs[:, 512:T])
            nc.scalar.activation(o[:, :, 512:T], tail[:], ACT.Sigmoid)
            for j in range(NT):
                cols = slice(j * P, (j + 1) * P)
                z = psum.tile([P, 512], F32, name="z", tag="z", bufs=2)
                matmul(z[:], words[:, cols], scales[:, cols], xw[:, 0:512], xs[:, 0:512])
                nc.scalar.activation(o[:, j, 0:512], z[:], ACT.Sigmoid)

        def fold_gate(j, r):
            nc.vector.tensor_tensor(og[:, j, r, :], o[:, j, :], g[:, r, :], MULT)

        def first_layer(e):
            stage = ring.tile([P, 1024], F32, name="b1", tag="b1", bufs=PRM["b1"], align_bytes=64)
            b = stage[:].bitcast(BF16)
            dst = b.rearrange("p (t m j) -> p m j t", t=4, j=4)
            src = raw1[e][:].rearrange("p j (m t) -> p m j t", t=4)
            split = PRM["m"][e]
            if split > 0:
                nc.scalar.copy(dst[:, 0:split], src[:, 0:split])
            if split < P:
                nc.vector.tensor_copy(dst[:, split:P], src[:, split:P])
            words = ring.tile([P, 512], U32, name="c1", tag="c1", bufs=PRM["c1"], align_bytes=64)
            scales = ring.tile([P, 512], U8, name="s1", tag="s1", bufs=PRM["c1"], align_bytes=64)
            quantize(words[:], scales[:], b)
            slots = slice(e * C, (e + 1) * C)
            hp = psum.tile([P, 4, C], F32, name="hp", tag="hp", bufs=2)
            for t in range(4):
                cols = slice(t * P, (t + 1) * P)
                matmul(hp[:, t, :], words[:, cols], scales[:, cols], xgw[:, slots], xgs[:, slots])
            hb = ring.tile([P, C, 4], BF16, name="hb", tag="hb", bufs=3, align_bytes=64)
            if PRM["relu"][e] == "scalar":
                nc.scalar.activation(hb[:], hp[:].rearrange("p t n -> p n t"), ACT.Relu)
            else:
                nc.vector.tensor_scalar_max(hb[:], hp[:].rearrange("p t n -> p n t"), 0.0)
            quantize(hw[:, slots], hs[:, slots], hb[:].rearrange("p n t -> p (n t)"))
            return stage

        def second_layer(k):
            pieces = groups[k]
            width = len(pieces) * P
            stage = ring.tile([P, 1024], F32, name="b1", tag="b1", bufs=PRM["b1"], align_bytes=64)
            b = stage[:, 0 : 2 * width].bitcast(BF16)
            dst = b.rearrange("p (c i j) -> p c j i", i=4, j=4)
            src = raw2[k][:, :, 0:width].rearrange("p j (c i) -> p c j i", i=4)
            split = PRM["f"][k] * width // (4 * 8)
            if split > 0:
                nc.scalar.copy(dst[:, 0:split], src[:, 0:split])
            if split < width // 4:
                nc.vector.tensor_copy(dst[:, split : width // 4], src[:, split : width // 4])
            words = ring.tile([P, width], U32, name="c1", tag="c1", bufs=PRM["c1"], align_bytes=64)
            scales = ring.tile([P, width], U8, name="s1", tag="s1", bufs=PRM["c1"], align_bytes=64)
            quantize(words[:], scales[:], b)
            yp = psum.tile([P, width], F32, name="yp", tag="yp", bufs=3)
            for i, piece in enumerate(pieces):
                cols = slice(i * P, (i + 1) * P)
                slots = slice(piece % E * C, (piece % E + 1) * C)
                matmul(yp[:, cols], words[:, cols], scales[:, cols], hw[:, slots], hs[:, slots])
            for j in sorted({piece // E for piece in pieces}):
                mine = [i for i, piece in enumerate(pieces) if piece // E == j]
                e0 = pieces[mine[0]] % E
                if j not in ys:
                    ys[j] = new_y()
                copy_on(
                    PRM["evac"][k],
                    ys[j][:, e0 * C : (e0 + len(mine)) * C],
                    yp[:, mine[0] * P : (mine[-1] + 1) * P],
                )
            return stage

        half = T // 2

        def combine(j, h, spent):
            tokens = slice(h * half, (h + 1) * half)
            if spent is None:
                spent = ring.tile([P, T], F32, name="parts", tag="parts", bufs=2)
            for r in range(2):
                lst = pos_t[r][:, h * half // 16 : (h + 1) * half // 16]
                nc.vector.tensor_tensor(
                    spent[:, r * half : (r + 1) * half], ys[j][:].indirect(lst), og[:, j, r, tokens], MULT
                )
            res = ring.tile([P, half], F32, name="res", tag="res", bufs=4)
            nc.vector.tensor_tensor(res[:], spent[:, 0:half], spent[:, half:T], ADD)
            nc.sync.dma_start(out[j * P : (j + 1) * P, tokens], res[:])

        def new_y():
            return ring.tile([P, S], F32, name="y", tag="y", bufs=3)

        ys = {}
        spent = []
        folds = [(j, r) for j in range(NT) for r in range(2)]
        for step in PRM["text"]:
            if step[0] == "x":
                gather_tokens(step[1])
            elif step[0] == "o":
                output_gate()
            elif step[0] == "a":
                spent.append(first_layer(step[1]))
            elif step[0] == "f":
                fold_gate(folds[step[1]][0], folds[step[1]][1])
            elif step[0] == "b":
                spent.append(second_layer(step[1]))
            elif step[0] == "c":
                combine(step[1] // 2, step[1] % 2, spent[-step[2]] if step[2] else None)
